import numpy as np, ml_dtypes
CORES = [19,147,275,403]
N = 4
import mx_ref
NC, G = 128, 2
C = np.float32(2.0 ** -4)
CNT = [[0,76,40,12],[12,0,76,40],[28,24,0,76],[88,28,12,0]]
OFF = [[sum(c[:e]) for e in range(N + 1)] for c in CNT]
BF = ml_dtypes.bfloat16
def cut(t, i, w=512):
    return t[:, w * i:w * i + w]
def tile(rs):
    return np.stack(rs, axis=2).reshape(128, -1).astype(BF)
def layer(w, X):
    out = []
    for i in range(G):
        for t in range(len(X)):
            p = mx_ref.matmul(mx_ref.quantize(cut(w, len(X) * i + t)), X[t])
            z = p if t == 0 else z + p
        out.append(z)
    return out
def gated(Z, g):
    return [(np.maximum(s * z, 0) * C) * g for z in Z for s in (1, -1)]
def setup_inputs(rng):
    def f(*shape):
        return mx_ref.flush((rng.standard_normal(shape, dtype=np.float32) * np.exp2(rng.integers(-2, 3, shape[:-1] + (1,)))).astype(BF))
    gt = np.broadcast_to((0.125 + 0.875 * rng.random((N, 1, NC))).astype(BF), (N, 128, NC)).copy()
    return {"gt": gt, "x": f(N, 128, 4 * NC), "w1": f(N, 128, G * 512), "w2": f(N, 128, 512)}
def setup_inputs_blocks(rng):
    d = setup_inputs(rng)
    for k in ("x", "w1", "w2"): d[k] = mx_ref.spread(d[k], rng, 4)
    return d
def setup_inputs_wide(rng):
    d = setup_inputs(rng)
    for k in ("x", "w1", "w2"): d[k] = mx_ref.flush((d[k].astype(np.float32) * np.exp2(rng.integers(-8, 9, (N, 1, 1))).astype(np.float32)).astype(BF))
    return d
def setup_inputs_zeros(rng):
    d = setup_inputs(rng); v = d["x"].reshape(N, 128, -1, 4).copy()
    v[np.broadcast_to((rng.random((N, 1, v.shape[2], 1)) < 0.33), v.shape)] = 0
    d["x"] = v.reshape(d["x"].shape)
    return d
def reference(gt, x, w1, w2):
    y = np.zeros((N, 128, NC), np.float32)
    for e in range(N):
        t = np.concatenate([x[j][:, 4 * OFF[j][e]:4 * OFF[j][e + 1]] for j in range(N)], axis=1)
        g = np.concatenate([gt[j][:, OFF[j][e]:OFF[j][e + 1]] for j in range(N)], axis=1).astype(np.float32)
        y[e] = mx_ref.matmul(mx_ref.quantize(w2[e]), mx_ref.quantize(tile(gated(layer(w1[e], [mx_ref.quantize(t)]), g))))
    return {"y": y}

@@ -1,0 +1,202 @@
+from concourse.bass import DstId, RemoteDMATransfer
+from concourse.mybir import dt, AluOpType, ActivationFunctionType
+
+NCOL = 128
+LO = 40
+SCRATCH = {
+    "xb": ("sbuf", [128, 512], "bfloat16"),
+    "qx": ("sbuf", [128, 128], "float8_e4m3fn_x4"),
+    "sx": ("sbuf", [128, 128], "uint8"),
+    "w1b": ("sbuf", [128, 1024], "bfloat16"),
+    "q1": ("sbuf", [128, 256], "float8_e4m3fn_x4"),
+    "s1": ("sbuf", [128, 256], "uint8"),
+    "w2b": ("sbuf", [128, 512], "bfloat16"),
+    "q2": ("sbuf", [128, 128], "float8_e4m3fn_x4"),
+    "s2": ("sbuf", [128, 128], "uint8"),
+    "bx": ("sbuf", [128, LO + NCOL], "float8_e4m3fn_x4"),
+    "bs": ("sbuf", [128, LO + NCOL], "uint8"),
+    "gd28": ("dram", [128, 28], "bfloat16"),
+    "gd40": ("dram", [128, 40], "bfloat16"),
+    "gdl": ("sbuf", [128, 40], "bfloat16"),
+    "gsrc": ("dram", [128, 2], "bfloat16"),
+    "gl": ("dram", [2, 128, 2], "bfloat16"),
+    "grow": ("sbuf", [1, NCOL], "bfloat16"),
+    "gg": ("sbuf", [128, NCOL], "bfloat16"),
+    "u": ("sbuf", [128, 2 * NCOL], "bfloat16"),
+    "h": ("sbuf", [128, 4 * NCOL], "bfloat16"),
+    "qh": ("sbuf", [128, 128], "float8_e4m3fn_x4"),
+    "sh": ("sbuf", [128, 128], "uint8"),
+    "yb": ("sbuf", [128, NCOL], "float32"),
+    "ps": ("psum", [128, 3 * 512], "float32"),
+}
+SEMAPHORES = ["ld_x", "ld_w", "ld_gd", "ld_gs", "v_x", "v_w", "a_c", "a_s", "arr", "sent", "h_gd", "gd", "tiny", "row",
+              "bc", "v_g", "z0", "z1", "u0", "u1", "h_s", "h_v", "v_h", "t_y", "v_y", "st"]
+
+
+def bits(mask):
+    return [1 << k for k in range(mask.bit_length()) if mask >> k & 1]
+
+
+def plan(T, topo):
+    C, n = T.cores, len(T.cores)
+    cnt = T.tables["CNT"]
+    off = [[sum(c[:e]) for e in range(n + 1)] for c in cnt]
+    far, via, bulk, helper = [], [], [], []
+    for i in range(n):
+        near = [j for j in range(n) if j != i and topo.may_write(C[i], C[j])]
+        far.append([j for j in range(n) if j != i and j not in near][0])
+        near.sort(key=lambda j: cnt[i][j])
+        via.append(near[0])
+        bulk.append(near[1])
+    for k in range(n):
+        target = far[bulk.index(k)]
+        first = [c for c in range(C[k] - C[k] % 8, C[k] - C[k] % 8 + 8)
+                 if topo.host(c) == topo.host(C[k]) and topo.chip(c) == topo.chip(C[k])
+                 and topo.die(c) != topo.die(C[k]) and topo.may_write(c, C[target])]
+        helper.append(first[0])
+    return cnt, off, far, via, bulk, helper
+
+
+def rank_program(g, core, T, topo):
+    C = T.cores
+    cnt, off, far, via, bulk, helper = plan(T, topo)
+    S = T.sem
+    rank = T.rank_of(core)
+
+    def cores_of(src, dst):
+        return len(bits(topo.mask(src, dst)))
+
+    def send(out, in_, dst, rsem):
+        rid, pid = topo.addr(dst, core)
+        m = topo.mask(core, dst)
+        g.remote_dma(out_ap=out, in_ap=in_, remote_sem=rsem, local_sem=S.sent, pid=pid, routing_id=rid, dma_engine_mask=m)
+        return len(bits(m))
+
+    if rank is None:
+        if core in helper:
+            s = bulk.index(helper.index(core))
+            w = cnt[s][far[s]]
+            g.wait_ge(S.h_gd, cores_of(C[s], core))
+            n = send(T.gdl[:, 0:w], T["gd%d" % w][:], C[far[s]], S.gd)
+            g.wait_ge(S.sent, n)
+        return
+
+    i = rank
+    f, v, b = far[i], via[i], bulk[i]
+    nf, nv, nb = cnt[i][f], cnt[i][v], cnt[i][b]
+    a_src, b_src = via.index(i), bulk.index(i)
+    own_a, own_c, own_b = cnt[a_src][i], cnt[f][i], cnt[b_src][i]
+    pass_n = cnt[a_src][far[a_src]]
+
+    def pieces(order):
+        out, pos = [], 0
+        for e in order:
+            if cnt[i][e]:
+                if out and out[-1][0] + out[-1][2] == off[i][e]:
+                    out[-1][2] += cnt[i][e]
+                else:
+                    out.append([off[i][e], pos, cnt[i][e]])
+            pos += cnt[i][e]
+        return out
+    order = min(([f, v, b], [b, f, v]), key=lambda o: len(pieces(o)))
+    at_a = 0 if order[0] == f else nb
+    at_b = nf + nv if order[0] == f else 0
+    load = pieces(order)
+
+    for k, (src, dst, n) in enumerate(load):
+        q = g.scalar if k else g.sync
+        q.dma_start(T.xb[:, 4 * dst:4 * (dst + n)], T.x[:, 4 * src:4 * (src + n)]).then_inc(S.ld_x, 16)
+    gd = T["gd%d" % nf]
+    g.scalar.dma_start(gd[:], T.gt[:, off[i][f]:off[i][f] + nf]).then_inc(S.ld_gd, 16)
+    g.scalar.dma_start(T.gsrc[:], T.gt[0:2, :]).then_inc(S.ld_gs, 16)
+    g.sync.dma_start(T.w1b[:], T.w1[:]).then_inc(S.ld_w, 16)
+    g.sync.dma_start(T.w2b[:], T.w2[:]).then_inc(S.ld_w, 16)
+
+    g.vector.wait_ge(S.ld_x, 16 * len(load))
+    g.vector.quantize_mx(T.qx[:], T.sx[:], T.xb[:]).then_inc(S.v_x, 1)
+    g.vector.wait_ge(S.ld_w, 32)
+    g.vector.quantize_mx(T.q1[:], T.s1[:], T.w1b[:]).then_inc(S.v_w, 1)
+    g.vector.quantize_mx(T.q2[:], T.s2[:], T.w2b[:]).then_inc(S.v_w, 1)
+
+    sent = 0
+    g.wait_ge(S.ld_gd, 16)
+    sent += send(gd[:], gd[:], helper[b], S.h_gd)
+    g.wait_ge(S.v_x, 1)
+    d0, d1 = LO - nf, LO + nv
+    sent += send(T.bx[:, d0:d1].bitcast(dt.uint8), T.qx[:, at_a:at_a + nf + nv].bitcast(dt.uint8), C[v], S.a_c)
+    sent += send(T.bs[:, d0:d1], T.sx[:, at_a:at_a + nf + nv], C[v], S.a_s)
+    g.wait_ge(S.ld_gs, 16)
+    tr = []
+    for k, d in ((0, v), (1, b)):
+        rid, pid = topo.addr(C[d], core)
+        tr.append(RemoteDMATransfer(dst_ids=[DstId(rid=rid, pnc=pid)], dma_engine_mask=bits(topo.mask(core, C[d]))[2 * k],
+                                    remote_sem=S.tiny, src=T.gsrc[:], dst=T.gl[k]))
+    g.remote_dma_fused(tr, local_sem=S.sent)
+    sent += 2
+    d0, d1 = LO + NCOL - nb, LO + NCOL
+    sent += send(T.bx[:, d0:d1].bitcast(dt.uint8), T.qx[:, at_b:at_b + nb].bitcast(dt.uint8), C[b], S.arr)
+    sent += send(T.bs[:, d0:d1], T.sx[:, at_b:at_b + nb], C[b], S.arr)
+    t = far[a_src]
+    d0 = LO + cnt[via.index(t)][t]
+    n_a = cores_of(C[a_src], core)
+    g.wait_ge(S.a_c, n_a)
+    sent += send(T.bx[:, d0:d0 + pass_n].bitcast(dt.uint8), T.bx[:, LO - pass_n:LO].bitcast(dt.uint8), C[t], S.arr)
+    g.wait_ge(S.a_s, n_a)
+    sent += send(T.bs[:, d0:d0 + pass_n], T.bs[:, LO - pass_n:LO], C[t], S.arr)
+
+    segs = ((0, a_src, 0, own_a), (1, b_src, own_a + own_c, own_b))
+    g.sync.wait_ge(S.tiny, 2)
+    for slot, s, pos, n in segs:
+        o = off[s][i]
+        g.sync.dma_start(T.grow[0:1, pos:pos + n], T.gl[slot, o // 2:(o + n) // 2, :]).then_inc(S.row, 16)
+    g.wait_ge(S.row, 32)
+    for slot, s, pos, n in segs:
+        g.partition_broadcast(T.gg[:, pos:pos + n], T.grow[0:1, pos:pos + n], 128).then_inc(S.bc, 1)
+    g.wait_ge(S.sent, sent)
+    g_from = helper[bulk[f]]
+    g.vector.wait_ge(S.gd, cores_of(g_from, core))
+    g.vector.tensor_copy(T.gg[:, own_a:own_a + own_c], T.gdl[:, 0:own_c]).then_inc(S.v_g, 1)
+
+    pe = g.tensor
+    pe.wait_ge(S.v_w, 2)
+    pe.wait_ge(S.a_c, n_a)
+    pe.wait_ge(S.a_s, n_a)
+    pe.wait_ge(S.arr, 2 * cores_of(C[b_src], core) + 2 * cores_of(C[via[f]], core))
+    for k, z in ((0, S.z0), (1, S.z1)):
+        pe.matmul_mx(T.ps[:, 512 * k:512 * k + NCOL], T.q1[:, 128 * k:128 * k + 128], T.s1[:, 128 * k:128 * k + 128],
+                     T.bx[:, LO:LO + NCOL], T.bs[:, LO:LO + NCOL], True, True).then_inc(z, 1)
+
+    g.vector.wait_ge(S.bc, 2)
+    g.vector.wait_ge(S.v_g, 1)
+    for k, z, us in ((0, S.z0, S.u0), (1, S.z1, S.u1)):
+        g.vector.wait_ge(z, 1)
+        g.vector.tensor_tensor(T.u[:, NCOL * k:NCOL * k + NCOL], T.ps[:, 512 * k:512 * k + NCOL], T.gg[:],
+                               AluOpType.mult).then_inc(us, 1)
+    g.scalar.wait_ge(S.u0, 1)
+    for r, c in ((0, 2.0 ** -4), (1, -2.0 ** -4)):
+        g.scalar.activation(T.h[:, r:4 * NCOL:4], T.u[:, 0:NCOL], ActivationFunctionType.Relu, scale=c).then_inc(S.h_s, 1)
+    g.vector.wait_ge(S.u1, 1)
+    for r, c in ((2, 2.0 ** -4), (3, -2.0 ** -4)):
+        g.vector.tensor_scalar(T.h[:, r:4 * NCOL:4], T.u[:, NCOL:2 * NCOL], c, 0.0, AluOpType.mult,
+                               AluOpType.max).then_inc(S.h_v, 1)
+    g.vector.wait_ge(S.h_v, 2)
+    g.vector.wait_ge(S.h_s, 2)
+    g.vector.quantize_mx(T.qh[:], T.sh[:], T.h[:]).then_inc(S.v_h, 1)
+
+    pe.wait_ge(S.v_h, 1)
+    pe.matmul_mx(T.ps[:, 1024:1024 + NCOL], T.q2[:], T.s2[:], T.qh[:], T.sh[:], True, True).then_inc(S.t_y, 1)
+    g.vector.wait_ge(S.t_y, 1)
+    win = {a_src: (0, own_a), f: (own_a, own_c), b_src: (own_a + own_c, own_b)}
+    cp, pos = [], 0
+    for j in sorted(win):
+        w0, n = win[j]
+        if cp and cp[-1][1] + cp[-1][2] == w0:
+            cp[-1][2] += n
+        else:
+            cp.append([pos, w0, n])
+        pos += n
+    for y0, w0, n in cp:
+        g.vector.tensor_copy(T.yb[:, y0:y0 + n], T.ps[:, 1024 + w0:1024 + w0 + n]).then_inc(S.v_y, 1)
+    g.sync.wait_ge(S.v_y, len(cp))
+    g.sync.dma_start(T.y[:], T.yb[:]).then_inc(S.st, 16)
+    g.sync.wait_ge(S.st, 16)

@@ -63,7 +63,7 @@ def rank_program(g, core, T, topo):
     S = T.sem
     rank = T.rank_of(core)
 
-    def cores_of(src, dst):
+    def engines(src, dst):
         return len(bits(topo.mask(src, dst)))
 
     def send(out, in_, dst, rsem):
@@ -76,7 +76,7 @@ def rank_program(g, core, T, topo):
         if core in helper:
             s = bulk.index(helper.index(core))
             w = cnt[s][far[s]]
-            g.wait_ge(S.h_gd, cores_of(C[s], core))
+            g.wait_ge(S.h_gd, engines(C[s], core))
             n = send(T.gdl[:, 0:w], T["gd%d" % w][:], C[far[s]], S.gd)
             g.wait_ge(S.sent, n)
         return
@@ -103,12 +103,12 @@ def rank_program(g, core, T, topo):
     at_b = nf + nv if order[0] == f else 0
     load = pieces(order)
 
+    g.scalar.dma_start(T.gsrc[:], T.gt[0:2, :]).then_inc(S.ld_gs, 16)
     for k, (src, dst, n) in enumerate(load):
         q = g.scalar if k else g.sync
         q.dma_start(T.xb[:, 4 * dst:4 * (dst + n)], T.x[:, 4 * src:4 * (src + n)]).then_inc(S.ld_x, 16)
     gd = T["gd%d" % nf]
     g.scalar.dma_start(gd[:], T.gt[:, off[i][f]:off[i][f] + nf]).then_inc(S.ld_gd, 16)
-    g.scalar.dma_start(T.gsrc[:], T.gt[0:2, :]).then_inc(S.ld_gs, 16)
     g.sync.dma_start(T.w1b[:], T.w1[:]).then_inc(S.ld_w, 16)
     g.sync.dma_start(T.w2b[:], T.w2[:]).then_inc(S.ld_w, 16)
 
@@ -119,33 +119,36 @@ def rank_program(g, core, T, topo):
     g.vector.quantize_mx(T.q2[:], T.s2[:], T.w2b[:]).then_inc(S.v_w, 1)
 
     sent = 0
+    g.wait_ge(S.ld_gs, 16)
+    tr = []
+    for k, d in ((0, v), (1, b)):
+        rid, pid = topo.addr(C[d], core)
+        mine = bits(topo.mask(core, C[d]))
+        half = len(mine) // 2
+        m = sum(mine[half * k:half * k + half])
+        tr.append(RemoteDMATransfer(dst_ids=[DstId(rid=rid, pnc=pid)], dma_engine_mask=m, remote_sem=S.tiny,
+                                    src=T.gsrc[:], dst=T.gl[k]))
+        sent += half
+    g.remote_dma_fused(tr, local_sem=S.sent)
     g.wait_ge(S.ld_gd, 16)
     sent += send(gd[:], gd[:], helper[b], S.h_gd)
     g.wait_ge(S.v_x, 1)
     d0, d1 = LO - nf, LO + nv
     sent += send(T.bx[:, d0:d1].bitcast(dt.uint8), T.qx[:, at_a:at_a + nf + nv].bitcast(dt.uint8), C[v], S.a_c)
     sent += send(T.bs[:, d0:d1], T.sx[:, at_a:at_a + nf + nv], C[v], S.a_s)
-    g.wait_ge(S.ld_gs, 16)
-    tr = []
-    for k, d in ((0, v), (1, b)):
-        rid, pid = topo.addr(C[d], core)
-        tr.append(RemoteDMATransfer(dst_ids=[DstId(rid=rid, pnc=pid)], dma_engine_mask=bits(topo.mask(core, C[d]))[2 * k],
-                                    remote_sem=S.tiny, src=T.gsrc[:], dst=T.gl[k]))
-    g.remote_dma_fused(tr, local_sem=S.sent)
-    sent += 2
     d0, d1 = LO + NCOL - nb, LO + NCOL
     sent += send(T.bx[:, d0:d1].bitcast(dt.uint8), T.qx[:, at_b:at_b + nb].bitcast(dt.uint8), C[b], S.arr)
     sent += send(T.bs[:, d0:d1], T.sx[:, at_b:at_b + nb], C[b], S.arr)
     t = far[a_src]
     d0 = LO + cnt[via.index(t)][t]
-    n_a = cores_of(C[a_src], core)
+    n_a = engines(C[a_src], core)
     g.wait_ge(S.a_c, n_a)
     sent += send(T.bx[:, d0:d0 + pass_n].bitcast(dt.uint8), T.bx[:, LO - pass_n:LO].bitcast(dt.uint8), C[t], S.arr)
     g.wait_ge(S.a_s, n_a)
     sent += send(T.bs[:, d0:d0 + pass_n], T.bs[:, LO - pass_n:LO], C[t], S.arr)
 
     segs = ((0, a_src, 0, own_a), (1, b_src, own_a + own_c, own_b))
-    g.sync.wait_ge(S.tiny, 2)
+    g.sync.wait_ge(S.tiny, engines(C[a_src], core) // 2 + engines(C[b_src], core) // 2)
     for slot, s, pos, n in segs:
         o = off[s][i]
         g.sync.dma_start(T.grow[0:1, pos:pos + n], T.gl[slot, o // 2:(o + n) // 2, :]).then_inc(S.row, 16)
@@ -153,15 +156,14 @@ def rank_program(g, core, T, topo):
     for slot, s, pos, n in segs:
         g.partition_broadcast(T.gg[:, pos:pos + n], T.grow[0:1, pos:pos + n], 128).then_inc(S.bc, 1)
     g.wait_ge(S.sent, sent)
-    g_from = helper[bulk[f]]
-    g.vector.wait_ge(S.gd, cores_of(g_from, core))
+    g.vector.wait_ge(S.gd, engines(helper[bulk[f]], core))
     g.vector.tensor_copy(T.gg[:, own_a:own_a + own_c], T.gdl[:, 0:own_c]).then_inc(S.v_g, 1)
 
     pe = g.tensor
     pe.wait_ge(S.v_w, 2)
     pe.wait_ge(S.a_c, n_a)
     pe.wait_ge(S.a_s, n_a)
-    pe.wait_ge(S.arr, 2 * cores_of(C[b_src], core) + 2 * cores_of(C[via[f]], core))
+    pe.wait_ge(S.arr, 2 * engines(C[b_src], core) + 2 * engines(C[via[f]], core))
     for k, z in ((0, S.z0), (1, S.z1)):
         pe.matmul_mx(T.ps[:, 512 * k:512 * k + NCOL], T.q1[:, 128 * k:128 * k + 128], T.s1[:, 128 * k:128 * k + 128],
                      T.bx[:, LO:LO + NCOL], T.bs[:, LO:LO + NCOL], True, True).then_inc(z, 1)

from concourse.bass import DstId, RemoteDMATransfer
from concourse.mybir import dt, AluOpType, ActivationFunctionType

NCOL = 128
LO = 40
SCRATCH = {
    "xb": ("sbuf", [128, 512], "bfloat16"),
    "qx": ("sbuf", [128, 128], "float8_e4m3fn_x4"),
    "sx": ("sbuf", [128, 128], "uint8"),
    "w1b": ("sbuf", [128, 1024], "bfloat16"),
    "q1": ("sbuf", [128, 256], "float8_e4m3fn_x4"),
    "s1": ("sbuf", [128, 256], "uint8"),
    "w2b": ("sbuf", [128, 512], "bfloat16"),
    "q2": ("sbuf", [128, 128], "float8_e4m3fn_x4"),
    "s2": ("sbuf", [128, 128], "uint8"),
    "bx": ("sbuf", [128, LO + NCOL], "float8_e4m3fn_x4"),
    "bs": ("sbuf", [128, LO + NCOL], "uint8"),
    "gd28": ("dram", [128, 28], "bfloat16"),
    "gd40": ("dram", [128, 40], "bfloat16"),
    "gdl": ("sbuf", [128, 40], "bfloat16"),
    "gsrc": ("dram", [128, 2], "bfloat16"),
    "gl": ("dram", [2, 128, 2], "bfloat16"),
    "grow": ("sbuf", [1, NCOL], "bfloat16"),
    "gg": ("sbuf", [128, NCOL], "bfloat16"),
    "u": ("sbuf", [128, 2 * NCOL], "bfloat16"),
    "h": ("sbuf", [128, 4 * NCOL], "bfloat16"),
    "qh": ("sbuf", [128, 128], "float8_e4m3fn_x4"),
    "sh": ("sbuf", [128, 128], "uint8"),
    "yb": ("sbuf", [128, NCOL], "float32"),
    "ps": ("psum", [128, 3 * 512], "float32"),
}
SEMAPHORES = ["ld_x", "ld_w", "ld_gd", "ld_gs", "v_x", "v_w", "a_c", "a_s", "arr", "sent", "h_gd", "gd", "tiny", "row",
              "bc", "v_g", "z0", "z1", "u0", "u1", "h_s", "h_v", "v_h", "t_y", "v_y", "st"]


def bits(mask):
    return [1 << k for k in range(mask.bit_length()) if mask >> k & 1]


def plan(T, topo):
    C, n = T.cores, len(T.cores)
    cnt = T.tables["CNT"]
    off = [[sum(c[:e]) for e in range(n + 1)] for c in cnt]
    far, via, bulk, helper = [], [], [], []
    for i in range(n):
        near = [j for j in range(n) if j != i and topo.may_write(C[i], C[j])]
        far.append([j for j in range(n) if j != i and j not in near][0])
        near.sort(key=lambda j: cnt[i][j])
        via.append(near[0])
        bulk.append(near[1])
    for k in range(n):
        target = far[bulk.index(k)]
        first = [c for c in range(C[k] - C[k] % 8, C[k] - C[k] % 8 + 8)
                 if topo.host(c) == topo.host(C[k]) and topo.chip(c) == topo.chip(C[k])
                 and topo.die(c) != topo.die(C[k]) and topo.may_write(c, C[target])]
        helper.append(first[0])
    return cnt, off, far, via, bulk, helper


def rank_program(g, core, T, topo):
    C = T.cores
    cnt, off, far, via, bulk, helper = plan(T, topo)
    S = T.sem
    rank = T.rank_of(core)

    def engines(src, dst):
        return len(bits(topo.mask(src, dst)))

    def send(out, in_, dst, rsem):
        rid, pid = topo.addr(dst, core)
        m = topo.mask(core, dst)
        g.remote_dma(out_ap=out, in_ap=in_, remote_sem=rsem, local_sem=S.sent, pid=pid, routing_id=rid, dma_engine_mask=m)
        return len(bits(m))

    if rank is None:
        if core in helper:
            s = bulk.index(helper.index(core))
            w = cnt[s][far[s]]
            g.wait_ge(S.h_gd, engines(C[s], core))
            n = send(T.gdl[:, 0:w], T["gd%d" % w][:], C[far[s]], S.gd)
            g.wait_ge(S.sent, n)
        return

    i = rank
    f, v, b = far[i], via[i], bulk[i]
    nf, nv, nb = cnt[i][f], cnt[i][v], cnt[i][b]
    a_src, b_src = via.index(i), bulk.index(i)
    own_a, own_c, own_b = cnt[a_src][i], cnt[f][i], cnt[b_src][i]
    pass_n = cnt[a_src][far[a_src]]

    def pieces(order):
        out, pos = [], 0
        for e in order:
            if cnt[i][e]:
                if out and out[-1][0] + out[-1][2] == off[i][e]:
                    out[-1][2] += cnt[i][e]
                else:
                    out.append([off[i][e], pos, cnt[i][e]])
            pos += cnt[i][e]
        return out
    order = min(([f, v, b], [b, f, v]), key=lambda o: len(pieces(o)))
    at_a = 0 if order[0] == f else nb
    at_b = nf + nv if order[0] == f else 0
    load = pieces(order)

    g.scalar.dma_start(T.gsrc[:], T.gt[0:2, :]).then_inc(S.ld_gs, 16)
    for k, (src, dst, n) in enumerate(load):
        q = g.scalar if k else g.sync
        q.dma_start(T.xb[:, 4 * dst:4 * (dst + n)], T.x[:, 4 * src:4 * (src + n)]).then_inc(S.ld_x, 16)
    gd = T["gd%d" % nf]
    g.scalar.dma_start(gd[:], T.gt[:, off[i][f]:off[i][f] + nf]).then_inc(S.ld_gd, 16)
    g.sync.dma_start(T.w1b[:], T.w1[:]).then_inc(S.ld_w, 16)
    g.sync.dma_start(T.w2b[:], T.w2[:]).then_inc(S.ld_w, 16)

    g.vector.wait_ge(S.ld_x, 16 * len(load))
    g.vector.quantize_mx(T.qx[:], T.sx[:], T.xb[:]).then_inc(S.v_x, 1)
    g.vector.wait_ge(S.ld_w, 32)
    g.vector.quantize_mx(T.q1[:], T.s1[:], T.w1b[:]).then_inc(S.v_w, 1)
    g.vector.quantize_mx(T.q2[:], T.s2[:], T.w2b[:]).then_inc(S.v_w, 1)

    sent = 0
    g.wait_ge(S.ld_gs, 16)
    tr = []
    for k, d in ((0, v), (1, b)):
        rid, pid = topo.addr(C[d], core)
        mine = bits(topo.mask(core, C[d]))
        half = len(mine) // 2
        m = sum(mine[half * k:half * k + half])
        tr.append(RemoteDMATransfer(dst_ids=[DstId(rid=rid, pnc=pid)], dma_engine_mask=m, remote_sem=S.tiny,
                                    src=T.gsrc[:], dst=T.gl[k]))
        sent += half
    g.remote_dma_fused(tr, local_sem=S.sent)
    g.wait_ge(S.ld_gd, 16)
    sent += send(gd[:], gd[:], helper[b], S.h_gd)
    g.wait_ge(S.v_x, 1)
    d0, d1 = LO - nf, LO + nv
    sent += send(T.bx[:, d0:d1].bitcast(dt.uint8), T.qx[:, at_a:at_a + nf + nv].bitcast(dt.uint8), C[v], S.a_c)
    sent += send(T.bs[:, d0:d1], T.sx[:, at_a:at_a + nf + nv], C[v], S.a_s)
    d0, d1 = LO + NCOL - nb, LO + NCOL
    sent += send(T.bx[:, d0:d1].bitcast(dt.uint8), T.qx[:, at_b:at_b + nb].bitcast(dt.uint8), C[b], S.arr)
    sent += send(T.bs[:, d0:d1], T.sx[:, at_b:at_b + nb], C[b], S.arr)
    t = far[a_src]
    d0 = LO + cnt[via.index(t)][t]
    n_a = engines(C[a_src], core)
    g.wait_ge(S.a_c, n_a)
    sent += send(T.bx[:, d0:d0 + pass_n].bitcast(dt.uint8), T.bx[:, LO - pass_n:LO].bitcast(dt.uint8), C[t], S.arr)
    g.wait_ge(S.a_s, n_a)
    sent += send(T.bs[:, d0:d0 + pass_n], T.bs[:, LO - pass_n:LO], C[t], S.arr)

    segs = ((0, a_src, 0, own_a), (1, b_src, own_a + own_c, own_b))
    g.sync.wait_ge(S.tiny, engines(C[a_src], core) // 2 + engines(C[b_src], core) // 2)
    for slot, s, pos, n in segs:
        o = off[s][i]
        g.sync.dma_start(T.grow[0:1, pos:pos + n], T.gl[slot, o // 2:(o + n) // 2, :]).then_inc(S.row, 16)
    g.wait_ge(S.row, 32)
    for slot, s, pos, n in segs:
        g.partition_broadcast(T.gg[:, pos:pos + n], T.grow[0:1, pos:pos + n], 128).then_inc(S.bc, 1)
    g.wait_ge(S.sent, sent)
    g.vector.wait_ge(S.gd, engines(helper[bulk[f]], core))
    g.vector.tensor_copy(T.gg[:, own_a:own_a + own_c], T.gdl[:, 0:own_c]).then_inc(S.v_g, 1)

    pe = g.tensor
    pe.wait_ge(S.v_w, 2)
    pe.wait_ge(S.a_c, n_a)
    pe.wait_ge(S.a_s, n_a)
    pe.wait_ge(S.arr, 2 * engines(C[b_src], core) + 2 * engines(C[via[f]], core))
    for k, z in ((0, S.z0), (1, S.z1)):
        pe.matmul_mx(T.ps[:, 512 * k:512 * k + NCOL], T.q1[:, 128 * k:128 * k + 128], T.s1[:, 128 * k:128 * k + 128],
                     T.bx[:, LO:LO + NCOL], T.bs[:, LO:LO + NCOL], True, True).then_inc(z, 1)

    g.vector.wait_ge(S.bc, 2)
    g.vector.wait_ge(S.v_g, 1)
    for k, z, us in ((0, S.z0, S.u0), (1, S.z1, S.u1)):
        g.vector.wait_ge(z, 1)
        g.vector.tensor_tensor(T.u[:, NCOL * k:NCOL * k + NCOL], T.ps[:, 512 * k:512 * k + NCOL], T.gg[:],
                               AluOpType.mult).then_inc(us, 1)
    g.scalar.wait_ge(S.u0, 1)
    for r, c in ((0, 2.0 ** -4), (1, -2.0 ** -4)):
        g.scalar.activation(T.h[:, r:4 * NCOL:4], T.u[:, 0:NCOL], ActivationFunctionType.Relu, scale=c).then_inc(S.h_s, 1)
    g.vector.wait_ge(S.u1, 1)
    for r, c in ((2, 2.0 ** -4), (3, -2.0 ** -4)):
        g.vector.tensor_scalar(T.h[:, r:4 * NCOL:4], T.u[:, NCOL:2 * NCOL], c, 0.0, AluOpType.mult,
                               AluOpType.max).then_inc(S.h_v, 1)
    g.vector.wait_ge(S.h_v, 2)
    g.vector.wait_ge(S.h_s, 2)
    g.vector.quantize_mx(T.qh[:], T.sh[:], T.h[:]).then_inc(S.v_h, 1)

    pe.wait_ge(S.v_h, 1)
    pe.matmul_mx(T.ps[:, 1024:1024 + NCOL], T.q2[:], T.s2[:], T.qh[:], T.sh[:], True, True).then_inc(S.t_y, 1)
    g.vector.wait_ge(S.t_y, 1)
    win = {a_src: (0, own_a), f: (own_a, own_c), b_src: (own_a + own_c, own_b)}
    cp, pos = [], 0
    for j in sorted(win):
        w0, n = win[j]
        if cp and cp[-1][1] + cp[-1][2] == w0:
            cp[-1][2] += n
        else:
            cp.append([pos, w0, n])
        pos += n
    for y0, w0, n in cp:
        g.vector.tensor_copy(T.yb[:, y0:y0 + n], T.ps[:, 1024 + w0:1024 + w0 + n]).then_inc(S.v_y, 1)
    g.sync.wait_ge(S.v_y, len(cp))
    g.sync.dma_start(T.y[:], T.yb[:]).then_inc(S.st, 16)
    g.sync.wait_ge(S.st, 16)
